import numpy as np, ml_dtypes
CORES = [16,17,18,19,32,33,34,35]
N = 8
import mx_ref
BF = ml_dtypes.bfloat16
def gentries(a):
    return np.ascontiguousarray(a.reshape(8, 16, -1).transpose(0, 2, 1)).reshape(8, -1)
def gtable(e):
    e = np.asarray(e); return np.ascontiguousarray(e.reshape(8, -1, 16).transpose(0, 2, 1)).reshape(128, -1).astype(np.int32)
def gcols(t, e):
    v = np.concatenate([t.reshape(8, 16, -1, 4), np.zeros((8, 16, 1, 4), BF)], axis=2)
    return np.ascontiguousarray(np.stack([v[g][:, e[g]] for g in range(8)])).reshape(128, -1)
def gpick(z, e):
    return np.concatenate([z[16 * g:16 * g + 16][:, e[g]] for g in range(8)])
def f(rng, *shape):
    return mx_ref.flush((rng.standard_normal(shape, dtype=np.float32) * np.exp2(rng.integers(-2, 3, shape[:-1] + (1,)))).astype(BF))
def wide(rng, *shape, cols=0):
    v = rng.standard_normal(shape, dtype=np.float32) * np.exp2(rng.integers(-12, 13, shape)).astype(np.float32)
    if cols: v *= np.repeat(np.exp2(rng.integers(-cols, cols + 1, shape[:-2] + (1, shape[-1] // 4))) * (rng.random(shape[:-2] + (1, shape[-1] // 4)) > 0.0625), 4, axis=-1).astype(np.float32)
    return mx_ref.flush(v.astype(BF))
T, CAPP, NB, KK = 1024, 96, 2, 512
MASK = np.repeat(np.arange(128)[:, None] // 16 == np.arange(128)[None] // 16, 4, axis=1)
def lists(rng, agree=False, one=False, full=False, repeat=False):
    a, o = [], []
    for r in range(N):
        n = rng.integers(0, CAPP + 1, (8, N))
        far, most, none = -1, -1, -1
        if one:
            far = (r + rng.integers(1, N)) % N; most, none = rng.permutation(8)[:2]
            n[most, far] = CAPP; n[none, far] = 0
        if full: n[:] = CAPP
        n[n.sum(axis=1) == 0, r] = 1
        e = np.full((8, N, CAPP), -1)
        for g in range(8):
            for q in range(N):
                v = rng.integers(0, T, n[g, q])
                if one and g == most and q == far: v = rng.permutation(T)[:CAPP]
                if full: v[0] = 0; v[1] = T - 1
                e[g, q, rng.permutation(CAPP)[:n[g, q]]] = v
        if agree: e = np.stack([e[0]] * 8)
        e = e.reshape(8, -1); used = [np.flatnonzero(e[g] >= 0) for g in range(8)]
        k = np.stack([np.full(KK, rng.choice(u)) if repeat else rng.choice(u, KK) for u in used])
        if one: k[most, rng.permutation(KK)[:CAPP]] = far * CAPP + rng.permutation(CAPP)
        if full: k[:, 0] = 0; k[:, -1] = N * CAPP - 1
        a.append(gtable(e)); o.append(gtable(k))
    return {"rq": np.stack(a), "od": np.stack(o)}
def setup_inputs(rng):
    ky = f(rng, N, 128, 4 * T); qd = np.array(f(rng, N, 128, NB * 512))
    qd[:, ~np.concatenate([MASK] * NB, axis=1)] = 0
    return {"ky": ky, "qd": qd, **lists(rng)}
def setup_inputs_agree(rng):
    return {**setup_inputs(rng), **lists(rng, agree=True)}
def setup_inputs_one(rng):
    return {**setup_inputs(rng), **lists(rng, one=True)}
def setup_inputs_full(rng):
    return {**setup_inputs(rng), **lists(rng, full=True)}
def setup_inputs_repeat(rng):
    return {**setup_inputs(rng), **lists(rng, repeat=True)}
def setup_inputs_spread(rng):
    d = setup_inputs(rng); d["ky"] = wide(rng, N, 128, 4 * T, cols=8); return d
def check_inputs(d):
    b = []
    for r in range(N):
        e, o = gentries(d["rq"][r]), gentries(d["od"][r])
        if e.min() < -1 or e.max() >= T: b.append("rq")
        if o.min() < 0 or o.max() >= N * CAPP or (np.take_along_axis(e, np.clip(o, 0, N * CAPP - 1), axis=1) < 0).any(): b.append("od")
        if not (d["qd"][r][~np.concatenate([MASK] * NB, axis=1)].astype(np.float32) == 0).all(): b.append("qd")
    return b
def reference(ky, qd, rq, od):
    y = np.zeros((N, 128, NB * KK), np.float32)
    for r in range(N):
        e, o = gentries(rq[r]), gentries(od[r])
        slots = mx_ref.quantize(np.concatenate([gcols(ky[q], e[:, q * CAPP:(q + 1) * CAPP]) for q in range(N)], axis=1))
        for b in range(NB):
            z = mx_ref.matmul(mx_ref.quantize(np.ascontiguousarray(qd[r][:, 512 * b:512 * b + 512])), slots)
            y[r][:, KK * b:KK * b + KK] = gpick(z, o)
    return {"y": y}

@@ -1,0 +1,244 @@
+from concourse.bass import DstId, RemoteDMATransfer
+from concourse.mybir import AluOpType, ActivationFunctionType
+
+N, CAPP, TK, NB, KK = 8, 96, 1024, 2, 512
+LW = CAPP // 16
+COPY = ActivationFunctionType.Copy
+
+SCRATCH = {
+    "rqsb": ("sbuf", [128, N * LW], "int32"),
+    "lst": ("sbuf", [128, (N - 1) * LW + 2], "int32"),
+    "kysb": ("sbuf", [128, 4 * TK], "bfloat16"),
+    "qdsb": ("sbuf", [128, NB * 512], "bfloat16"),
+    "odsb": ("sbuf", [128, KK // 16], "int32"),
+    "odof": ("sbuf", [128, KK // 16], "uint16"),
+    "tile": ("sbuf", [128, 4 * (N - 1) * CAPP], "bfloat16"),
+    "tself": ("sbuf", [128, 4 * 128], "bfloat16"),
+    "qc": ("sbuf", [128, (N - 1) * CAPP], "float8_e4m3fn_x4"),
+    "qp": ("sbuf", [128, (N - 1) * CAPP], "uint8"),
+    "sc": ("sbuf", [128, 128], "float8_e4m3fn_x4"),
+    "sp": ("sbuf", [128, 128], "uint8"),
+    "dc": ("sbuf", [128, NB * 128], "float8_e4m3fn_x4"),
+    "dp": ("sbuf", [128, NB * 128], "uint8"),
+    "onc": ("sbuf", [128, 3 * CAPP], "float8_e4m3fn_x4"),
+    "onp": ("sbuf", [128, 3 * CAPP], "uint8"),
+    "ofc": ("sbuf", [128, 4 * CAPP], "float8_e4m3fn_x4"),
+    "ofp": ("sbuf", [128, 4 * CAPP], "uint8"),
+    "z0": ("sbuf", [128, N * CAPP], "float32"),
+    "z1": ("sbuf", [128, N * CAPP], "float32"),
+    "y0": ("sbuf", [128, KK], "float32"),
+    "y1": ("sbuf", [128, KK], "float32"),
+    "ps": ("psum", [128, 512 * 6], "float32"),
+}
+for _t in range(4):
+    SCRATCH["off%d" % _t] = ("sbuf", [128, (N - 1) * LW], "uint16")
+    SCRATCH["sof%d" % _t] = ("sbuf", [128, LW], "uint16")
+
+SEMAPHORES = (["ld_rq", "ld_ky", "ld_qd", "ld_od", "lists", "sent", "arr_on", "arr_off", "qd_q", "self_q", "odv", "zero"]
+              + ["soff", "sself", "vself"]
+              + ["o%d" % t for t in range(4)]
+              + ["vg%d" % c for c in range(3)] + ["sg%d" % c for c in range(3)] + ["q%d" % c for c in range(3)]
+              + ["mm_%s%d" % (k, b) for k in ("self", "on", "off") for b in range(2)]
+              + ["cp0", "cp1"] + ["gy%d%d" % (b, h) for b in range(2) for h in range(2)] + ["st"])
+
+
+def rank_program(g, core, T, topo):
+    rank = T.rank_of(core)
+    if rank is None:
+        return
+    cores = T.cores
+
+    def on_chip(r):
+        return [q for q in range(N) if topo.chip(cores[q]) == topo.chip(cores[r])]
+
+    def off_chip(r):
+        return [q for q in range(N) if topo.chip(cores[q]) != topo.chip(cores[r])]
+
+    def order(r):
+        i = on_chip(r).index(r)
+        off = off_chip(r)
+        first = off[:2] if i < 2 else off[2:]
+        second = [q for q in off if q not in first]
+        return [first, second, [q for q in on_chip(r) if q != r]]
+
+    mine = order(rank)
+    flat = mine[0] + mine[1] + mine[2]
+    far = mine[0] + mine[1]
+    near = mine[2]
+    e_far = topo.engines(core, cores[far[0]])
+    e_near = [e for e in topo.engines(core, cores[near[0]]) if e not in e_far]
+
+    def bits(es):
+        return sum(1 << e for e in es)
+
+    def send(dst, mask, sem, src, out):
+        rid, pid, _ = topo.addr(cores[dst])
+        return RemoteDMATransfer(dst_ids=[DstId(rid=rid, pnc=pid)], dma_engine_mask=mask,
+                                 remote_sem=sem, srcs=[src], dsts=[out])
+
+    def deal(dsts, engines, per):
+        return {d: bits(engines[per * k:per * k + per]) for k, d in enumerate(dsts)}
+
+    U8 = _u8()
+    pos = {d: k for k, d in enumerate(flat)}
+
+    def theirs(d):
+        o = order(d)
+        return (o[0] + o[1] + o[2]).index(rank)
+
+    def codes(d, near_side):
+        a = CAPP * pos[d]
+        if near_side:
+            b = CAPP * [q for q in on_chip(d) if q != d].index(rank)
+            return T.qc[:, a:a + CAPP].bitcast(U8), T.onc[:, b:b + CAPP].bitcast(U8)
+        b = CAPP * off_chip(d).index(rank)
+        return T.qc[:, a:a + CAPP].bitcast(U8), T.ofc[:, b:b + CAPP].bitcast(U8)
+
+    def planes(d, near_side):
+        a = CAPP * pos[d]
+        if near_side:
+            b = CAPP * [q for q in on_chip(d) if q != d].index(rank)
+            return T.qp[:, a:a + CAPP], T.onp[:, b:b + CAPP]
+        b = CAPP * off_chip(d).index(rank)
+        return T.qp[:, a:a + CAPP], T.ofp[:, b:b + CAPP]
+
+    S = T.sem
+    n_lists = 2 * (N - 1)
+
+    g.sync.dma_start(T.rqsb[:], T.rq[:]).then_inc(S.ld_rq, 16)
+    g.sync.dma_start(T.kysb[:], T.ky[:]).then_inc(S.ld_ky, 16)
+    g.sync.wait_ge(S.lists, n_lists)
+    g.sync.dma_start(T.qdsb[:], T.qd[:]).then_inc(S.ld_qd, 16)
+    g.sync.dma_start(T.odsb[:], T.od[:]).then_inc(S.ld_od, 16)
+
+    m_far2, m_near2 = deal(far, e_far, 2), deal(near, e_near, 2)
+    g.wait_ge(S.ld_rq, 16)
+    tr = []
+    for d in flat:
+        m = m_far2[d] if d in m_far2 else m_near2[d]
+        k = LW * theirs(d)
+        tr.append(send(d, m, S.lists, T.rqsb[:, LW * d:LW * d + LW], T.lst[:, k:k + LW]))
+    g.remote_dma_fused(tr, local_sem=S.sent)
+    sent = n_lists
+    for c in range(2):
+        g.wait_ge(S["q%d" % c], 1)
+        m = deal(mine[c], e_far, 4)
+        g.remote_dma_fused([send(d, m[d], S.arr_off, *codes(d, False)) for d in mine[c]], local_sem=S.sent)
+        sent += 8
+    g.remote_dma_fused([send(d, m_far2[d], S.arr_off, *planes(d, False)) for d in far], local_sem=S.sent)
+    sent += 8
+    g.wait_ge(S.q2, 1)
+    g.remote_dma_fused([send(d, m_near2[d], S.arr_on, *codes(d, True)) for d in near], local_sem=S.sent)
+    g.remote_dma_fused([send(d, m_near2[d], S.arr_on, *planes(d, True)) for d in near], local_sem=S.sent)
+    sent += 12
+    g.wait_ge(S.sent, sent)
+
+    V, A = g.vector, g.scalar
+    V.memset(T.tself[:, 4 * CAPP:4 * 128], 0.0).then_inc(S.zero, 1)
+    V.wait_ge(S.ld_rq, 16)
+    for t in range(4):
+        V.tensor_scalar(T["sof%d" % t][:], T.rqsb[:, LW * rank:LW * rank + LW], 4, t,
+                        AluOpType.mult, AluOpType.add).then_inc(S.soff, 1)
+    V.wait_ge(S.lists, n_lists)
+    for t in range(4):
+        V.tensor_scalar(T["off%d" % t][:], T.lst[:, 0:(N - 1) * LW], 4, t,
+                        AluOpType.mult, AluOpType.add).then_inc(S["o%d" % t], 1)
+    V.wait_ge(S.ld_ky, 16)
+    A.wait_ge(S.ld_ky, 16)
+    win = T.kysb[:, 0:4 * TK]
+    a = 0
+    for c in range(3):
+        n = CAPP * len(mine[c])
+        l0, l1 = a // 16, (a + n) // 16
+        for t in (0, 1):
+            if c == 0:
+                A.wait_ge(S["o%d" % t], 1)
+            A.activation(T.tile[:, 4 * a + t:4 * (a + n):4], win.indirect(T["off%d" % t][:, l0:l1]), COPY
+                         ).then_inc(S["sg%d" % c], 1)
+        for t in (2, 3):
+            if c == 0:
+                V.wait_ge(S["o%d" % t], 1)
+            V.tensor_copy(T.tile[:, 4 * a + t:4 * (a + n):4], win.indirect(T["off%d" % t][:, l0:l1])
+                          ).then_inc(S["vg%d" % c], 1)
+        V.wait_ge(S["vg%d" % c], 2)
+        V.wait_ge(S["sg%d" % c], 2)
+        V.quantize_mx(T.qc[:, a:a + n], T.qp[:, a:a + n], T.tile[:, 4 * a:4 * (a + n)]).then_inc(S["q%d" % c], 1)
+        a += n
+    A.wait_ge(S.soff, 4)
+    V.wait_ge(S.soff, 4)
+    for t in (0, 1):
+        A.activation(T.tself[:, t:4 * CAPP:4], win.indirect(T["sof%d" % t][:]), COPY).then_inc(S.sself, 1)
+    for t in (2, 3):
+        V.tensor_copy(T.tself[:, t:4 * CAPP:4], win.indirect(T["sof%d" % t][:])).then_inc(S.vself, 1)
+    V.wait_ge(S.ld_qd, 16)
+    V.quantize_mx(T.dc[:], T.dp[:], T.qdsb[:]).then_inc(S.qd_q, 1)
+    V.wait_ge(S.zero, 1)
+    V.wait_ge(S.vself, 2)
+    V.wait_ge(S.sself, 2)
+    V.quantize_mx(T.sc[:], T.sp[:], T.tself[:]).then_inc(S.self_q, 1)
+    V.wait_ge(S.ld_od, 16)
+    V.tensor_copy(T.odof[:], T.odsb[:]).then_inc(S.odv, 1)
+
+    P = g.tensor
+
+    def products(k, rc, rp, n, name):
+        for b in range(NB):
+            o = 512 * (2 * k + b)
+            P.matmul_mx(T.ps[:, o:o + n], T.dc[:, 128 * b:128 * b + 128], T.dp[:, 128 * b:128 * b + 128],
+                        rc[:, 0:n], rp[:, 0:n], True, True).then_inc(S["mm_%s%d" % (name, b)], 1)
+
+    P.wait_ge(S.qd_q, 1)
+    P.wait_ge(S.self_q, 1)
+    products(0, T.sc, T.sp, 128, "self")
+    P.wait_ge(S.arr_on, 2 * 2 * len(near))
+    products(1, T.onc, T.onp, CAPP * len(near), "on")
+    P.wait_ge(S.arr_off, 4 * len(far) + 2 * len(far))
+    products(2, T.ofc, T.ofp, CAPP * len(far), "off")
+
+    def copies(b, put):
+        z = T["z%d" % b]
+        n = 0
+        g_wait = (V if b == 0 else A).wait_ge
+        g_wait(S["mm_self%d" % b], 1)
+        o = 512 * b
+        put(z[:, CAPP * rank:CAPP * rank + CAPP], T.ps[:, o:o + CAPP])
+        n += 1
+        g_wait(S["mm_on%d" % b], 1)
+        o = 512 * (2 + b)
+        low = [q for q in near if q < rank]
+        high = [q for q in near if q > rank]
+        for part, first in ((low, 0), (high, len(low))):
+            if part:
+                w = CAPP * len(part)
+                put(z[:, CAPP * part[0]:CAPP * part[0] + w], T.ps[:, o + CAPP * first:o + CAPP * first + w])
+                n += 1
+        g_wait(S["mm_off%d" % b], 1)
+        o = 512 * (4 + b)
+        w = CAPP * len(far)
+        f0 = CAPP * min(far)
+        put(z[:, f0:f0 + w], T.ps[:, o:o + w])
+        n += 1
+        g_wait(S["cp%d" % b], n)
+        g_wait(S.odv, 1)
+
+    copies(0, lambda out, src: V.tensor_copy(out, src).then_inc(S.cp0, 1))
+    copies(1, lambda out, src: A.activation(out, src, COPY).then_inc(S.cp1, 1))
+    half = KK // 2
+    hl = half // 16
+    for h in range(2):
+        V.tensor_copy(T.y0[:, half * h:half * h + half], T.z0[:].indirect(T.odof[:, hl * h:hl * h + hl])
+                      ).then_inc(S["gy0%d" % h], 1)
+        A.activation(T.y1[:, half * h:half * h + half], T.z1[:].indirect(T.odof[:, hl * h:hl * h + hl]), COPY
+                     ).then_inc(S["gy1%d" % h], 1)
+    for h in range(2):
+        for b in range(2):
+            q = A if (b == 1 and h == 1) else g.sync
+            q.wait_ge(S["gy%d%d" % (b, h)], 1)
+            q.dma_start(T.y[:, KK * b + half * h:KK * b + half * h + half],
+                        T["y%d" % b][:, half * h:half * h + half]).then_inc(S.st, 16)
+    g.sync.wait_ge(S.st, 64)
+
+
+def _u8():
+    from concourse.mybir import dt
+    return dt.uint8

@@ -1,52 +1,53 @@
 from concourse.bass import DstId, RemoteDMATransfer
-from concourse.mybir import AluOpType, ActivationFunctionType
+from concourse.mybir import AluOpType, ActivationFunctionType, dt
 
 N, CAPP, TK, NB, KK = 8, 96, 1024, 2, 512
 LW = CAPP // 16
 COPY = ActivationFunctionType.Copy
+U8 = dt.uint8
+NF, NN = 4, 3
 
 SCRATCH = {
     "rqsb": ("sbuf", [128, N * LW], "int32"),
-    "lst": ("sbuf", [128, (N - 1) * LW + 2], "int32"),
+    "lst": ("sbuf", [128, (N - 1) * LW], "int32"),
     "kysb": ("sbuf", [128, 4 * TK], "bfloat16"),
     "qdsb": ("sbuf", [128, NB * 512], "bfloat16"),
     "odsb": ("sbuf", [128, KK // 16], "int32"),
     "odof": ("sbuf", [128, KK // 16], "uint16"),
-    "tile": ("sbuf", [128, 4 * (N - 1) * CAPP], "bfloat16"),
-    "tself": ("sbuf", [128, 4 * 128], "bfloat16"),
-    "qc": ("sbuf", [128, (N - 1) * CAPP], "float8_e4m3fn_x4"),
-    "qp": ("sbuf", [128, (N - 1) * CAPP], "uint8"),
-    "sc": ("sbuf", [128, 128], "float8_e4m3fn_x4"),
-    "sp": ("sbuf", [128, 128], "uint8"),
+    "tile": ("sbuf", [128, 4 * N * CAPP], "bfloat16"),
+    "qc": ("sbuf", [128, N * CAPP], "float8_e4m3fn_x4"),
+    "qp": ("sbuf", [128, N * CAPP], "uint8"),
     "dc": ("sbuf", [128, NB * 128], "float8_e4m3fn_x4"),
     "dp": ("sbuf", [128, NB * 128], "uint8"),
-    "onc": ("sbuf", [128, 3 * CAPP], "float8_e4m3fn_x4"),
-    "onp": ("sbuf", [128, 3 * CAPP], "uint8"),
-    "ofc": ("sbuf", [128, 4 * CAPP], "float8_e4m3fn_x4"),
-    "ofp": ("sbuf", [128, 4 * CAPP], "uint8"),
+    "onc": ("sbuf", [128, NN * CAPP], "float8_e4m3fn_x4"),
+    "onp": ("sbuf", [128, NN * CAPP], "uint8"),
+    "ofc": ("sbuf", [128, NF * CAPP], "float8_e4m3fn_x4"),
+    "ofp": ("sbuf", [128, NF * CAPP], "uint8"),
+    "hlst": ("sbuf", [128, LW], "int32"),
+    "hpl": ("sbuf", [128, NF * CAPP], "uint8"),
     "z0": ("sbuf", [128, N * CAPP], "float32"),
     "z1": ("sbuf", [128, N * CAPP], "float32"),
     "y0": ("sbuf", [128, KK], "float32"),
     "y1": ("sbuf", [128, KK], "float32"),
-    "ps": ("psum", [128, 512 * 6], "float32"),
+    "ps": ("psum", [128, 512 * 8], "float32"),
 }
 for _t in range(4):
-    SCRATCH["off%d" % _t] = ("sbuf", [128, (N - 1) * LW], "uint16")
-    SCRATCH["sof%d" % _t] = ("sbuf", [128, LW], "uint16")
+    SCRATCH["off%d" % _t] = ("sbuf", [128, N * LW], "uint16")
 
-SEMAPHORES = (["ld_rq", "ld_ky", "ld_qd", "ld_od", "lists", "sent", "arr_on", "arr_off", "qd_q", "self_q", "odv", "zero"]
-              + ["soff", "sself", "vself"]
-              + ["o%d" % t for t in range(4)]
-              + ["vg%d" % c for c in range(3)] + ["sg%d" % c for c in range(3)] + ["q%d" % c for c in range(3)]
-              + ["mm_%s%d" % (k, b) for k in ("self", "on", "off") for b in range(2)]
+CHUNKS = ((0, 128, 0), (128, 256, 96), (384, 192, 64), (576, 192, 0))
+LAST = 3
+PIECES = ((0, 192), (192, KK))
+
+SEMAPHORES = (["ld_rq", "ld_ky", "ld_qd", "ld_od", "lists", "list2", "hl", "hp", "sent", "arr_on", "arr_off", "qd_q",
+               "odv", "soff"]
+              + ["o%d" % t for t in range(4)] + ["p%d" % t for t in range(4)]
+              + ["%s%d" % (k, c) for k in ("vg", "sg", "q") for c in range(4)]
+              + ["mm_%s%d" % (k, b) for k in ("self", "on", "offa", "offb") for b in range(2)]
               + ["cp0", "cp1"] + ["gy%d%d" % (b, h) for b in range(2) for h in range(2)] + ["st"])
 
 
 def rank_program(g, core, T, topo):
-    rank = T.rank_of(core)
-    if rank is None:
-        return
-    cores = T.cores
+    cores, S = T.cores, T.sem
 
     def on_chip(r):
         return [q for q in range(N) if topo.chip(cores[q]) == topo.chip(cores[r])]
@@ -54,191 +55,205 @@ def rank_program(g, core, T, topo):
     def off_chip(r):
         return [q for q in range(N) if topo.chip(cores[q]) != topo.chip(cores[r])]
 
-    def order(r):
-        i = on_chip(r).index(r)
-        off = off_chip(r)
-        first = off[:2] if i < 2 else off[2:]
-        second = [q for q in off if q not in first]
-        return [first, second, [q for q in on_chip(r) if q != r]]
+    def far_of(r):
+        i, o = on_chip(r).index(r), off_chip(r)
+        return o[i:] + o[:i]
 
-    mine = order(rank)
-    flat = mine[0] + mine[1] + mine[2]
-    far = mine[0] + mine[1]
-    near = mine[2]
-    e_far = topo.engines(core, cores[far[0]])
-    e_near = [e for e in topo.engines(core, cores[near[0]]) if e not in e_far]
+    def near_of(r):
+        i, o = on_chip(r).index(r), on_chip(r)
+        return o[i + 1:] + o[:i]
+
+    def helper_of(r):
+        other = [c for c in topo.cores_of(cores[r]) if topo.die(c) != topo.die(cores[r])]
+        return other[on_chip(r).index(r)]
 
     def bits(es):
         return sum(1 << e for e in es)
 
     def send(dst, mask, sem, src, out):
-        rid, pid, _ = topo.addr(cores[dst])
+        rid, pid, _ = topo.addr(dst)
         return RemoteDMATransfer(dst_ids=[DstId(rid=rid, pnc=pid)], dma_engine_mask=mask,
                                  remote_sem=sem, srcs=[src], dsts=[out])
 
-    def deal(dsts, engines, per):
-        return {d: bits(engines[per * k:per * k + per]) for k, d in enumerate(dsts)}
+    def list_place(r, d):
+        k = LW * (far_of(d) + near_of(d)).index(r)
+        return T.lst[:, k:k + LW]
 
-    U8 = _u8()
-    pos = {d: k for k, d in enumerate(flat)}
+    def off_place(buf, r, d):
+        k = CAPP * off_chip(d).index(r)
+        return buf[:, k:k + CAPP]
 
-    def theirs(d):
-        o = order(d)
-        return (o[0] + o[1] + o[2]).index(rank)
+    def on_place(buf, r, d):
+        k = CAPP * [q for q in on_chip(d) if q != d].index(r)
+        return buf[:, k:k + CAPP]
 
-    def codes(d, near_side):
-        a = CAPP * pos[d]
-        if near_side:
-            b = CAPP * [q for q in on_chip(d) if q != d].index(rank)
-            return T.qc[:, a:a + CAPP].bitcast(U8), T.onc[:, b:b + CAPP].bitcast(U8)
-        b = CAPP * off_chip(d).index(rank)
-        return T.qc[:, a:a + CAPP].bitcast(U8), T.ofc[:, b:b + CAPP].bitcast(U8)
+    rank = T.rank_of(core)
+    if rank is None:
+        for r in range(N):
+            if helper_of(r) == core:
+                helper(g, T, r, core, topo, far_of(r), near_of(r)[0], bits, send, list_place, off_place)
+        return
 
-    def planes(d, near_side):
-        a = CAPP * pos[d]
-        if near_side:
-            b = CAPP * [q for q in on_chip(d) if q != d].index(rank)
-            return T.qp[:, a:a + CAPP], T.onp[:, b:b + CAPP]
-        b = CAPP * off_chip(d).index(rank)
-        return T.qp[:, a:a + CAPP], T.ofp[:, b:b + CAPP]
+    far, near = far_of(rank), near_of(rank)
+    e_far = topo.engines(core, cores[far[0]])
+    e_near = [e for e in topo.engines(core, cores[near[0]]) if e not in e_far]
+    m_all = bits(e_near)
+    half_n = len(e_near) // 2
 
-    S = T.sem
-    n_lists = 2 * (N - 1)
-
+    direct = 2 * (N - 2)
     g.sync.dma_start(T.rqsb[:], T.rq[:]).then_inc(S.ld_rq, 16)
     g.sync.dma_start(T.kysb[:], T.ky[:]).then_inc(S.ld_ky, 16)
-    g.sync.wait_ge(S.lists, n_lists)
+    g.sync.wait_ge(S.lists, direct)
     g.sync.dma_start(T.qdsb[:], T.qd[:]).then_inc(S.ld_qd, 16)
     g.sync.dma_start(T.odsb[:], T.od[:]).then_inc(S.ld_od, 16)
 
-    m_far2, m_near2 = deal(far, e_far, 2), deal(near, e_near, 2)
+    def piece(buf, k, n=CAPP):
+        return buf[:, CAPP * k:CAPP * k + n]
+
+    def far_codes(k, mask):
+        d = far[k]
+        return send(cores[d], mask, S.arr_off, piece(T.qc, k).bitcast(U8), off_place(T.ofc, rank, d).bitcast(U8))
+
+    def near_codes(k, mask):
+        d = near[k]
+        return send(cores[d], mask, S.arr_on, piece(T.qc, NF + k).bitcast(U8), on_place(T.onc, rank, d).bitcast(U8))
+
+    def near_planes(k, mask):
+        d = near[k]
+        return send(cores[d], mask, S.arr_on, piece(T.qp, NF + k), on_place(T.onp, rank, d))
+
     g.wait_ge(S.ld_rq, 16)
     tr = []
-    for d in flat:
-        m = m_far2[d] if d in m_far2 else m_near2[d]
-        k = LW * theirs(d)
-        tr.append(send(d, m, S.lists, T.rqsb[:, LW * d:LW * d + LW], T.lst[:, k:k + LW]))
+    for k, d in enumerate(far):
+        tr.append(send(cores[d], bits(e_far[2 * k:2 * k + 2]), S.lists,
+                       T.rqsb[:, LW * d:LW * d + LW], list_place(rank, d)))
+    for k, d in enumerate(near):
+        src, mask = T.rqsb[:, LW * d:LW * d + LW], bits(e_near[2 * k:2 * k + 2])
+        if k == 0:
+            tr.append(send(helper_of(rank) if True else None, mask, S.hl, src, T.hlst[:]))
+        else:
+            tr.append(send(cores[d], mask, S.lists, src, list_place(rank, d)))
     g.remote_dma_fused(tr, local_sem=S.sent)
-    sent = n_lists
-    for c in range(2):
-        g.wait_ge(S["q%d" % c], 1)
-        m = deal(mine[c], e_far, 4)
-        g.remote_dma_fused([send(d, m[d], S.arr_off, *codes(d, False)) for d in mine[c]], local_sem=S.sent)
-        sent += 8
-    g.remote_dma_fused([send(d, m_far2[d], S.arr_off, *planes(d, False)) for d in far], local_sem=S.sent)
-    sent += 8
+    g.wait_ge(S.q0, 1)
+    g.remote_dma_fused([far_codes(0, bits(e_far))], local_sem=S.sent)
+    g.wait_ge(S.q1, 1)
+    g.remote_dma_fused([far_codes(1, bits(e_far[0:4])), far_codes(2, bits(e_far[4:6])), far_codes(3, bits(e_far[6:8])),
+                        send(helper_of(rank), m_all, S.hp, piece(T.qp, 0, NF * CAPP), T.hpl[:])], local_sem=S.sent)
     g.wait_ge(S.q2, 1)
-    g.remote_dma_fused([send(d, m_near2[d], S.arr_on, *codes(d, True)) for d in near], local_sem=S.sent)
-    g.remote_dma_fused([send(d, m_near2[d], S.arr_on, *planes(d, True)) for d in near], local_sem=S.sent)
-    sent += 12
-    g.wait_ge(S.sent, sent)
+    g.remote_dma_fused([near_codes(0, bits(e_near[:half_n])), near_codes(1, bits(e_near[half_n:]))], local_sem=S.sent)
+    g.wait_ge(S.q3, 1)
+    g.remote_dma_fused([near_codes(2, m_all)], local_sem=S.sent)
+    g.remote_dma_fused([near_planes(0, bits(e_near[0:2])), near_planes(1, bits(e_near[2:4])),
+                        near_planes(2, bits(e_near[4:8]))], local_sem=S.sent)
+    g.wait_ge(S.sent, 2 * (N - 1) + 8 + 16 + 8 + 8 + 8)
 
     V, A = g.vector, g.scalar
-    V.memset(T.tself[:, 4 * CAPP:4 * 128], 0.0).then_inc(S.zero, 1)
+
+    def offsets(dst0, src, w, names):
+        for t in range(4):
+            V.tensor_scalar(T["off%d" % t][:, dst0:dst0 + w], src, 4, t,
+                            AluOpType.mult, AluOpType.add).then_inc(S[names[t]], 1)
+
     V.wait_ge(S.ld_rq, 16)
-    for t in range(4):
-        V.tensor_scalar(T["sof%d" % t][:], T.rqsb[:, LW * rank:LW * rank + LW], 4, t,
-                        AluOpType.mult, AluOpType.add).then_inc(S.soff, 1)
-    V.wait_ge(S.lists, n_lists)
-    for t in range(4):
-        V.tensor_scalar(T["off%d" % t][:], T.lst[:, 0:(N - 1) * LW], 4, t,
-                        AluOpType.mult, AluOpType.add).then_inc(S["o%d" % t], 1)
+    offsets((N - 1) * LW, T.rqsb[:, LW * rank:LW * rank + LW], LW, ["soff"] * 4)
+    V.wait_ge(S.lists, direct)
+    w1 = (N - 2) * LW
+    offsets(0, T.lst[:, 0:w1], w1, ["o%d" % t for t in range(4)])
     V.wait_ge(S.ld_ky, 16)
+    V.wait_ge(S.o2, 1)
+    V.wait_ge(S.o3, 1)
     A.wait_ge(S.ld_ky, 16)
+    A.wait_ge(S.o0, 1)
+    A.wait_ge(S.o1, 1)
     win = T.kysb[:, 0:4 * TK]
-    a = 0
-    for c in range(3):
-        n = CAPP * len(mine[c])
-        l0, l1 = a // 16, (a + n) // 16
-        for t in (0, 1):
-            if c == 0:
-                A.wait_ge(S["o%d" % t], 1)
-            A.activation(T.tile[:, 4 * a + t:4 * (a + n):4], win.indirect(T["off%d" % t][:, l0:l1]), COPY
-                         ).then_inc(S["sg%d" % c], 1)
-        for t in (2, 3):
-            if c == 0:
-                V.wait_ge(S["o%d" % t], 1)
-            V.tensor_copy(T.tile[:, 4 * a + t:4 * (a + n):4], win.indirect(T["off%d" % t][:, l0:l1])
-                          ).then_inc(S["vg%d" % c], 1)
+    for c, (a, n, s) in enumerate(CHUNKS):
+        if c == 1:
+            A.wait_ge(S.o2, 1)
+        if c == LAST:
+            V.wait_ge(S.list2, 8)
+            offsets(w1, T.lst[:, w1:w1 + LW], LW, ["p%d" % t for t in range(4)])
+            for q, ts in ((V, (2, 3)), (A, (0, 1))):
+                q.wait_ge(S.soff, 4)
+                for t in ts:
+                    q.wait_ge(S["p%d" % t], 1)
+        for t, b, m in [(0, a, n), (1, a, n)] + ([(2, a, s)] if s else []):
+            A.activation(T.tile[:, 4 * b + t:4 * (b + m):4],
+                         win.indirect(T["off%d" % t][:, b // 16:(b + m) // 16]), COPY).then_inc(S["sg%d" % c], 1)
+        for t, b, m in [(2, a + s, n - s), (3, a, n)]:
+            V.tensor_copy(T.tile[:, 4 * b + t:4 * (b + m):4],
+                          win.indirect(T["off%d" % t][:, b // 16:(b + m) // 16])).then_inc(S["vg%d" % c], 1)
         V.wait_ge(S["vg%d" % c], 2)
-        V.wait_ge(S["sg%d" % c], 2)
+        V.wait_ge(S["sg%d" % c], 3 if s else 2)
         V.quantize_mx(T.qc[:, a:a + n], T.qp[:, a:a + n], T.tile[:, 4 * a:4 * (a + n)]).then_inc(S["q%d" % c], 1)
-        a += n
-    A.wait_ge(S.soff, 4)
-    V.wait_ge(S.soff, 4)
-    for t in (0, 1):
-        A.activation(T.tself[:, t:4 * CAPP:4], win.indirect(T["sof%d" % t][:]), COPY).then_inc(S.sself, 1)
-    for t in (2, 3):
-        V.tensor_copy(T.tself[:, t:4 * CAPP:4], win.indirect(T["sof%d" % t][:])).then_inc(S.vself, 1)
     V.wait_ge(S.ld_qd, 16)
     V.quantize_mx(T.dc[:], T.dp[:], T.qdsb[:]).then_inc(S.qd_q, 1)
-    V.wait_ge(S.zero, 1)
-    V.wait_ge(S.vself, 2)
-    V.wait_ge(S.sself, 2)
-    V.quantize_mx(T.sc[:], T.sp[:], T.tself[:]).then_inc(S.self_q, 1)
     V.wait_ge(S.ld_od, 16)
     V.tensor_copy(T.odof[:], T.odsb[:]).then_inc(S.odv, 1)
 
     P = g.tensor
 
-    def products(k, rc, rp, n, name):
+    def products(k, rc, rp, c0, n, name):
         for b in range(NB):
             o = 512 * (2 * k + b)
             P.matmul_mx(T.ps[:, o:o + n], T.dc[:, 128 * b:128 * b + 128], T.dp[:, 128 * b:128 * b + 128],
-                        rc[:, 0:n], rp[:, 0:n], True, True).then_inc(S["mm_%s%d" % (name, b)], 1)
+                        rc[:, c0:c0 + n], rp[:, c0:c0 + n], True, True).then_inc(S["mm_%s%d" % (name, b)], 1)
 
+    w_off = CAPP * NF // 2
+    lead = 128 - CAPP
+    P.wait_ge(S["q%d" % LAST], 1)
     P.wait_ge(S.qd_q, 1)
-    P.wait_ge(S.self_q, 1)
-    products(0, T.sc, T.sp, 128, "self")
-    P.wait_ge(S.arr_on, 2 * 2 * len(near))
-    products(1, T.onc, T.onp, CAPP * len(near), "on")
-    P.wait_ge(S.arr_off, 4 * len(far) + 2 * len(far))
-    products(2, T.ofc, T.ofp, CAPP * len(far), "off")
+    products(0, T.qc, T.qp, N * CAPP - 128, 128, "self")
+    P.wait_ge(S.arr_on, 4 + 4 + 8 + 2 + 2 + 4)
+    products(1, T.onc, T.onp, 0, CAPP * NN, "on")
+    P.wait_ge(S.arr_off, 8 + 4 + 2 + 2 + 2 * NF)
+    products(2, T.ofc, T.ofp, 0, w_off, "offa")
+    products(3, T.ofc, T.ofp, w_off, w_off, "offb")
 
-    def copies(b, put):
+    def copies(b, wait, put):
         z = T["z%d" % b]
-        n = 0
-        g_wait = (V if b == 0 else A).wait_ge
-        g_wait(S["mm_self%d" % b], 1)
-        o = 512 * b
+        n = 1
+        wait(S["mm_self%d" % b], 1)
+        o = 512 * b + lead
         put(z[:, CAPP * rank:CAPP * rank + CAPP], T.ps[:, o:o + CAPP])
-        n += 1
-        g_wait(S["mm_on%d" % b], 1)
+        wait(S["mm_on%d" % b], 1)
         o = 512 * (2 + b)
-        low = [q for q in near if q < rank]
-        high = [q for q in near if q > rank]
+        low = [q for q in sorted(near) if q < rank]
+        high = [q for q in sorted(near) if q > rank]
         for part, first in ((low, 0), (high, len(low))):
             if part:
                 w = CAPP * len(part)
                 put(z[:, CAPP * part[0]:CAPP * part[0] + w], T.ps[:, o + CAPP * first:o + CAPP * first + w])
                 n += 1
-        g_wait(S["mm_off%d" % b], 1)
-        o = 512 * (4 + b)
-        w = CAPP * len(far)
         f0 = CAPP * min(far)
-        put(z[:, f0:f0 + w], T.ps[:, o:o + w])
-        n += 1
-        g_wait(S["cp%d" % b], n)
-        g_wait(S.odv, 1)
+        for k, name in ((2, "offa"), (3, "offb")):
+            wait(S["mm_%s%d" % (name, b)], 1)
+            o = 512 * (2 * k + b)
+            put(z[:, f0:f0 + w_off], T.ps[:, o:o + w_off])
+            f0 += w_off
+            n += 1
+        wait(S["cp%d" % b], n)
+        wait(S.odv, 1)
 
-    copies(0, lambda out, src: V.tensor_copy(out, src).then_inc(S.cp0, 1))
-    copies(1, lambda out, src: A.activation(out, src, COPY).then_inc(S.cp1, 1))
-    half = KK // 2
-    hl = half // 16
-    for h in range(2):
-        V.tensor_copy(T.y0[:, half * h:half * h + half], T.z0[:].indirect(T.odof[:, hl * h:hl * h + hl])
-                      ).then_inc(S["gy0%d" % h], 1)
-        A.activation(T.y1[:, half * h:half * h + half], T.z1[:].indirect(T.odof[:, hl * h:hl * h + hl]), COPY
-                     ).then_inc(S["gy1%d" % h], 1)
-    for h in range(2):
+    copies(0, V.wait_ge, lambda out, src: V.tensor_copy(out, src).then_inc(S.cp0, 1))
+    copies(1, A.wait_ge, lambda out, src: A.activation(out, src, COPY).then_inc(S.cp1, 1))
+    for h, (k0, k1) in enumerate(PIECES):
+        picks = T.odof[:, k0 // 16:k1 // 16]
+        V.tensor_copy(T.y0[:, k0:k1], T.z0[:].indirect(picks)).then_inc(S["gy0%d" % h], 1)
+        A.activation(T.y1[:, k0:k1], T.z1[:].indirect(picks), COPY).then_inc(S["gy1%d" % h], 1)
+    for h, (k0, k1) in enumerate(PIECES):
         for b in range(2):
             q = A if (b == 1 and h == 1) else g.sync
             q.wait_ge(S["gy%d%d" % (b, h)], 1)
-            q.dma_start(T.y[:, KK * b + half * h:KK * b + half * h + half],
-                        T["y%d" % b][:, half * h:half * h + half]).then_inc(S.st, 16)
+            q.dma_start(T.y[:, KK * b + k0:KK * b + k1], T["y%d" % b][:, k0:k1]).then_inc(S.st, 16)
     g.sync.wait_ge(S.st, 64)
 
 
-def _u8():
-    from concourse.mybir import dt
-    return dt.uint8
+def helper(g, T, r, core, topo, far, peer, bits, send, list_place, off_place):
+    cores, S = T.cores, T.sem
+    es = topo.engines(core, cores[far[0]])
+    g.wait_ge(S.hl, 2)
+    g.remote_dma_fused([send(cores[peer], bits(es), S.list2, T.hlst[:], list_place(r, peer))], local_sem=S.sent)
+    g.wait_ge(S.hp, 8)
+    g.remote_dma_fused([send(cores[d], bits(es[2 * k:2 * k + 2]), S.arr_off, T.hpl[:, CAPP * k:CAPP * k + CAPP],
+                             off_place(T.ofp, r, d)) for k, d in enumerate(far)], local_sem=S.sent)
+    g.wait_ge(S.sent, 8 + 8)

@@ -6,6 +6,24 @@ LW = CAPP // 16
 COPY = ActivationFunctionType.Copy
 U8 = dt.uint8
 NF, NN = 4, 3
+PAIR = 2 * CAPP
+PAD = 128 - CAPP
+PADC = (N - 1) * CAPP
+OWN = PADC + PAD
+COLS = OWN + CAPP + PAD
+
+TILE = ["f0", "f2", "f1", "f3", "n0", "n1", "n2"]
+CHUNKS = ((0, 192, 64), (192, 192, 64), (384, 192, 64), (576, 128, 0))
+STAGES = {0: (0, 4, "la"), 2: (4, 6, "lb"), 3: (6, 7, "lh")}
+LISTS = [[("f0", "f0.2"), ("f1", "f2.2"), ("f2", "f4.2"), ("f3", "f6.2")],
+         [("n0", "n0.2"), ("n1", "n2.2"), ("n2", "n4.4")]]
+CALLS = [(0, [("hc", 0, "n0.8"), ("fc", 2, "f0.8")]), (0, [("hp", 0, "n0.8"), ("fp", 2, "f0.8")]),
+         (1, [("hc", 1, "n0.8"), ("fc", 3, "f0.8")]), (1, [("fp", 1, "f0.4"), ("fp", 3, "f4.4")]),
+         (2, [("nc", 0, "n0.4"), ("nc", 1, "n4.4")]), (2, [("np", 0, "n0.4"), ("np", 1, "n4.4")]),
+         (3, [("nc", 2, "n0.8")]), (3, [("np", 2, "n0.8")])]
+HELP = [("hc0", [("fc", 0, "f0.8")]), ("hp0", [("fp", 0, "f0.8")]), ("hc1", [("fc", 1, "f0.8")])]
+PRODUCTS = "nmba"
+PIECES = ((0, 160), (160, KK))
 
 SCRATCH = {
     "rqsb": ("sbuf", [128, N * LW], "int32"),
@@ -14,17 +32,18 @@ SCRATCH = {
     "qdsb": ("sbuf", [128, NB * 512], "bfloat16"),
     "odsb": ("sbuf", [128, KK // 16], "int32"),
     "odof": ("sbuf", [128, KK // 16], "uint16"),
-    "tile": ("sbuf", [128, 4 * N * CAPP], "bfloat16"),
-    "qc": ("sbuf", [128, N * CAPP], "float8_e4m3fn_x4"),
-    "qp": ("sbuf", [128, N * CAPP], "uint8"),
+    "tile": ("sbuf", [128, 4 * COLS], "bfloat16"),
+    "qc": ("sbuf", [128, PADC + PAD], "float8_e4m3fn_x4"),
+    "qp": ("sbuf", [128, PADC + PAD], "uint8"),
     "dc": ("sbuf", [128, NB * 128], "float8_e4m3fn_x4"),
     "dp": ("sbuf", [128, NB * 128], "uint8"),
-    "onc": ("sbuf", [128, NN * CAPP], "float8_e4m3fn_x4"),
-    "onp": ("sbuf", [128, NN * CAPP], "uint8"),
+    "onc": ("sbuf", [128, 2 * PAIR + PAD], "float8_e4m3fn_x4"),
+    "onp": ("sbuf", [128, 2 * PAIR + PAD], "uint8"),
     "ofc": ("sbuf", [128, NF * CAPP], "float8_e4m3fn_x4"),
     "ofp": ("sbuf", [128, NF * CAPP], "uint8"),
     "hlst": ("sbuf", [128, LW], "int32"),
-    "hpl": ("sbuf", [128, NF * CAPP], "uint8"),
+    "hcd": ("sbuf", [128, PAIR], "float8_e4m3fn_x4"),
+    "hpl": ("sbuf", [128, PAIR], "uint8"),
     "z0": ("sbuf", [128, N * CAPP], "float32"),
     "z1": ("sbuf", [128, N * CAPP], "float32"),
     "y0": ("sbuf", [128, KK], "float32"),
@@ -34,16 +53,12 @@ SCRATCH = {
 for _t in range(4):
     SCRATCH["off%d" % _t] = ("sbuf", [128, N * LW], "uint16")
 
-CHUNKS = ((0, 128, 0), (128, 256, 96), (384, 192, 64), (576, 192, 0))
-LAST = 3
-PIECES = ((0, 192), (192, KK))
-
-SEMAPHORES = (["ld_rq", "ld_ky", "ld_qd", "ld_od", "lists", "list2", "hl", "hp", "sent", "arr_on", "arr_off", "qd_q",
-               "odv", "soff"]
-              + ["o%d" % t for t in range(4)] + ["p%d" % t for t in range(4)]
-              + ["%s%d" % (k, c) for k in ("vg", "sg", "q") for c in range(4)]
-              + ["mm_%s%d" % (k, b) for k in ("self", "on", "offa", "offb") for b in range(2)]
-              + ["cp0", "cp1"] + ["gy%d%d" % (b, h) for b in range(2) for h in range(2)] + ["st"])
+SEMAPHORES = (["ld_rq", "ld_ky", "ld_qd", "ld_od", "la", "lb", "lh", "hl", "hc0", "hc1", "hp0", "sent",
+               "arr_n", "arr_m", "arr_a", "arr_b", "qd_q", "odv", "pad", "q_own", "v_own", "s_own"]
+              + ["%s%d" % (k, t) for k in ("so", "la_", "lb_", "lh_") for t in range(4)]
+              + ["%s%d" % (k, c) for k in ("vg", "sg", "q") for c in range(len(CHUNKS))]
+              + ["mm_%s%d" % (k, b) for k in "nmab" for b in range(NB)]
+              + ["cp0", "cp1"] + ["gy%d%d" % (b, h) for b in range(NB) for h in range(2)] + ["st"])
 
 
 def rank_program(g, core, T, topo):
@@ -57,203 +72,205 @@ def rank_program(g, core, T, topo):
 
     def far_of(r):
         i, o = on_chip(r).index(r), off_chip(r)
-        return o[i:] + o[:i]
+        return [o[i ^ k] for k in range(NF)]
 
     def near_of(r):
         i, o = on_chip(r).index(r), on_chip(r)
-        return o[i + 1:] + o[:i]
+        return [o[i ^ k] for k in (2, 3, 1)]
+
+    def peer(r, name):
+        return (far_of(r) if name[0] == "f" else near_of(r))[int(name[1])]
 
     def helper_of(r):
         other = [c for c in topo.cores_of(cores[r]) if topo.die(c) != topo.die(cores[r])]
         return other[on_chip(r).index(r)]
 
-    def bits(es):
-        return sum(1 << e for e in es)
+    rank = T.rank_of(core)
+    mine = [r for r in range(N) if helper_of(r) == core]
+    if rank is None and not mine:
+        return
+    home = mine[0] if rank is None else rank
+    far, near = far_of(home), near_of(home)
 
-    def send(dst, mask, sem, src, out):
+    pool = {"f": topo.engines(core, cores[far[0]])}
+    pool["n"] = [e for e in topo.engines(core, cores[near[0]]) if e not in pool["f"]]
+
+    def count(es):
+        return int(es.split(".")[1])
+
+    sent = [0]
+
+    def send(dst, es, sem, src, out):
+        first, n = int(es[1:].split(".")[0]), count(es)
         rid, pid, _ = topo.addr(dst)
-        return RemoteDMATransfer(dst_ids=[DstId(rid=rid, pnc=pid)], dma_engine_mask=mask,
-                                 remote_sem=sem, srcs=[src], dsts=[out])
+        sent[0] += n
+        return RemoteDMATransfer(dst_ids=[DstId(rid=rid, pnc=pid)],
+                                 dma_engine_mask=sum(1 << e for e in pool[es[0]][first:first + n]),
+                                 remote_sem=S[sem], srcs=[src], dsts=[out])
 
     def list_place(r, d):
-        k = LW * (far_of(d) + near_of(d)).index(r)
+        k = LW * [peer(d, x) for x in TILE].index(r)
         return T.lst[:, k:k + LW]
 
-    def off_place(buf, r, d):
-        k = CAPP * off_chip(d).index(r)
-        return buf[:, k:k + CAPP]
+    def own_place(d):
+        return (OWN, PAIR + CAPP) if near_of(d)[2] < d else (PADC, PAIR)
 
-    def on_place(buf, r, d):
-        k = CAPP * [q for q in on_chip(d) if q != d].index(r)
-        return buf[:, k:k + CAPP]
+    def place(kind, r, d):
+        if kind[0] == "f":
+            k = CAPP * off_chip(d).index(r)
+        elif r == near_of(d)[2]:
+            k = PAIR if r < d else PAIR + PAD + CAPP
+        else:
+            k = CAPP * sorted(near_of(d)[:2]).index(r)
+        return T["o" + kind][:, k:k + CAPP]
 
-    rank = T.rank_of(core)
+    def u8(kind, ap):
+        return ap.bitcast(U8) if kind[1] == "c" else ap
+
+    def arrival(kind, k):
+        if kind[0] == "h":
+            return "%s%d" % (kind, k)
+        return "arr_" + (("m" if k == 2 else "n") if kind[0] == "n" else "a" if k < 2 else "b")
+
+    due = {}
+    for _, tr in CALLS + HELP:
+        for kind, k, es in tr:
+            due[arrival(kind, k)] = due.get(arrival(kind, k), 0) + count(es)
+    due["la"] = sum(count(es) for x, es in LISTS[0])
+    due["lb"] = sum(count(es) for x, es in LISTS[1][:2])
+    due["hl"] = count(LISTS[1][2][1])
+    due["lh"] = len(pool["f"])
+
     if rank is None:
-        for r in range(N):
-            if helper_of(r) == core:
-                helper(g, T, r, core, topo, far_of(r), near_of(r)[0], bits, send, list_place, off_place)
+        d = near[NN - 1]
+        g.wait_ge(S.hl, due["hl"])
+        g.remote_dma_fused([send(cores[d], "f0.%d" % due["lh"], "lh", T.hlst[:], list_place(home, d))], local_sem=S.sent)
+        for sem, tr in HELP:
+            g.wait_ge(S[sem], due[sem])
+            g.remote_dma_fused([send(cores[far[k]], es, arrival(kind, k),
+                                     u8(kind, (T.hcd if kind == "fc" else T.hpl)[:, CAPP * k:CAPP * k + CAPP]),
+                                     u8(kind, place(kind, home, far[k]))) for kind, k, es in tr], local_sem=S.sent)
+        g.wait_ge(S.sent, sent[0])
         return
+    helper = helper_of(rank)
 
-    far, near = far_of(rank), near_of(rank)
-    e_far = topo.engines(core, cores[far[0]])
-    e_near = [e for e in topo.engines(core, cores[near[0]]) if e not in e_far]
-    m_all = bits(e_near)
-    half_n = len(e_near) // 2
-
-    direct = 2 * (N - 2)
     g.sync.dma_start(T.rqsb[:], T.rq[:]).then_inc(S.ld_rq, 16)
     g.sync.dma_start(T.kysb[:], T.ky[:]).then_inc(S.ld_ky, 16)
-    g.sync.wait_ge(S.lists, direct)
+    g.sync.wait_ge(S.la, due["la"])
     g.sync.dma_start(T.qdsb[:], T.qd[:]).then_inc(S.ld_qd, 16)
     g.sync.dma_start(T.odsb[:], T.od[:]).then_inc(S.ld_od, 16)
 
-    def piece(buf, k, n=CAPP):
-        return buf[:, CAPP * k:CAPP * k + n]
+    def list_send(x, es, sem):
+        d = peer(rank, x)
+        src = T.rqsb[:, LW * d:LW * d + LW]
+        if x == TILE[-1]:
+            return send(helper, es, "hl", src, T.hlst[:])
+        return send(cores[d], es, sem, src, list_place(rank, d))
 
-    def far_codes(k, mask):
-        d = far[k]
-        return send(cores[d], mask, S.arr_off, piece(T.qc, k).bitcast(U8), off_place(T.ofc, rank, d).bitcast(U8))
-
-    def near_codes(k, mask):
-        d = near[k]
-        return send(cores[d], mask, S.arr_on, piece(T.qc, NF + k).bitcast(U8), on_place(T.onc, rank, d).bitcast(U8))
-
-    def near_planes(k, mask):
-        d = near[k]
-        return send(cores[d], mask, S.arr_on, piece(T.qp, NF + k), on_place(T.onp, rank, d))
+    def data_send(kind, k, es):
+        buf = T.qc if kind[1] == "c" else T.qp
+        name = "%s%d" % ("n" if kind[0] == "n" else "f", k)
+        a = CAPP * TILE.index(name)
+        src = u8(kind, buf[:, a:a + CAPP])
+        if kind[0] == "h":
+            out = (T.hcd if kind == "hc" else T.hpl)[:, CAPP * k:CAPP * k + CAPP]
+            return send(helper, es, arrival(kind, k), src, u8(kind, out))
+        d = peer(rank, name)
+        return send(cores[d], es, arrival(kind, k), src, u8(kind, place(kind, rank, d)))
 
     g.wait_ge(S.ld_rq, 16)
-    tr = []
-    for k, d in enumerate(far):
-        tr.append(send(cores[d], bits(e_far[2 * k:2 * k + 2]), S.lists,
-                       T.rqsb[:, LW * d:LW * d + LW], list_place(rank, d)))
-    for k, d in enumerate(near):
-        src, mask = T.rqsb[:, LW * d:LW * d + LW], bits(e_near[2 * k:2 * k + 2])
-        if k == 0:
-            tr.append(send(helper_of(rank) if True else None, mask, S.hl, src, T.hlst[:]))
-        else:
-            tr.append(send(cores[d], mask, S.lists, src, list_place(rank, d)))
-    g.remote_dma_fused(tr, local_sem=S.sent)
-    g.wait_ge(S.q0, 1)
-    g.remote_dma_fused([far_codes(0, bits(e_far))], local_sem=S.sent)
-    g.wait_ge(S.q1, 1)
-    g.remote_dma_fused([far_codes(1, bits(e_far[0:4])), far_codes(2, bits(e_far[4:6])), far_codes(3, bits(e_far[6:8])),
-                        send(helper_of(rank), m_all, S.hp, piece(T.qp, 0, NF * CAPP), T.hpl[:])], local_sem=S.sent)
-    g.wait_ge(S.q2, 1)
-    g.remote_dma_fused([near_codes(0, bits(e_near[:half_n])), near_codes(1, bits(e_near[half_n:]))], local_sem=S.sent)
-    g.wait_ge(S.q3, 1)
-    g.remote_dma_fused([near_codes(2, m_all)], local_sem=S.sent)
-    g.remote_dma_fused([near_planes(0, bits(e_near[0:2])), near_planes(1, bits(e_near[2:4])),
-                        near_planes(2, bits(e_near[4:8]))], local_sem=S.sent)
-    g.wait_ge(S.sent, 2 * (N - 1) + 8 + 16 + 8 + 8 + 8)
+    for row, sem in zip(LISTS, ("la", "lb")):
+        g.remote_dma_fused([list_send(x, es, sem) for x, es in row], local_sem=S.sent)
+    for c, tr in CALLS:
+        g.wait_ge(S["q%d" % c], 1)
+        g.remote_dma_fused([data_send(*x) for x in tr], local_sem=S.sent)
+    g.wait_ge(S.sent, sent[0])
 
     V, A = g.vector, g.scalar
-
-    def offsets(dst0, src, w, names):
-        for t in range(4):
-            V.tensor_scalar(T["off%d" % t][:, dst0:dst0 + w], src, 4, t,
-                            AluOpType.mult, AluOpType.add).then_inc(S[names[t]], 1)
-
-    V.wait_ge(S.ld_rq, 16)
-    offsets((N - 1) * LW, T.rqsb[:, LW * rank:LW * rank + LW], LW, ["soff"] * 4)
-    V.wait_ge(S.lists, direct)
-    w1 = (N - 2) * LW
-    offsets(0, T.lst[:, 0:w1], w1, ["o%d" % t for t in range(4)])
-    V.wait_ge(S.ld_ky, 16)
-    V.wait_ge(S.o2, 1)
-    V.wait_ge(S.o3, 1)
-    A.wait_ge(S.ld_ky, 16)
-    A.wait_ge(S.o0, 1)
-    A.wait_ge(S.o1, 1)
     win = T.kysb[:, 0:4 * TK]
+
+    def offsets(col, src, w, name):
+        for t in range(4):
+            V.tensor_scalar(T["off%d" % t][:, col:col + w], src, 4, t,
+                            AluOpType.mult, AluOpType.add).then_inc(S["%s%d" % (name, t)], 1)
+
+    def gather(q, t, a, col, n, sem):
+        out, src = T.tile[:, 4 * a + t:4 * (a + n):4], win.indirect(T["off%d" % t][:, col:col + n // 16])
+        if q is V:
+            V.tensor_copy(out, src).then_inc(S[sem], 1)
+        else:
+            A.activation(out, src, COPY).then_inc(S[sem], 1)
+
+    for a in (PADC, OWN + CAPP):
+        V.memset(T.tile[:, 4 * a:4 * (a + PAD)], 0.0).then_inc(S.pad, 1)
+    V.wait_ge(S.ld_rq, 16)
+    offsets((N - 1) * LW, T.rqsb[:, LW * rank:LW * rank + LW], LW, "so")
+    V.wait_ge(S.pad, 2)
     for c, (a, n, s) in enumerate(CHUNKS):
-        if c == 1:
-            A.wait_ge(S.o2, 1)
-        if c == LAST:
-            V.wait_ge(S.list2, 8)
-            offsets(w1, T.lst[:, w1:w1 + LW], LW, ["p%d" % t for t in range(4)])
-            for q, ts in ((V, (2, 3)), (A, (0, 1))):
-                q.wait_ge(S.soff, 4)
-                for t in ts:
-                    q.wait_ge(S["p%d" % t], 1)
-        for t, b, m in [(0, a, n), (1, a, n)] + ([(2, a, s)] if s else []):
-            A.activation(T.tile[:, 4 * b + t:4 * (b + m):4],
-                         win.indirect(T["off%d" % t][:, b // 16:(b + m) // 16]), COPY).then_inc(S["sg%d" % c], 1)
-        for t, b, m in [(2, a + s, n - s), (3, a, n)]:
-            V.tensor_copy(T.tile[:, 4 * b + t:4 * (b + m):4],
-                          win.indirect(T["off%d" % t][:, b // 16:(b + m) // 16])).then_inc(S["vg%d" % c], 1)
+        if c in STAGES:
+            k0, k1, sem = STAGES[c]
+            V.wait_ge(S[sem], due[sem])
+            offsets(LW * k0, T.lst[:, LW * k0:LW * k1], LW * (k1 - k0), sem + "_")
+        if c == 0:
+            V.wait_ge(S.ld_ky, 16)
+            A.wait_ge(S.ld_ky, 16)
+        m = min(a + n, PADC) - a
+        for q, jobs, done in ((A, [(0, a, m), (1, a, m)] + ([(2, a, s)] if s else []), "sg%d" % c),
+                              (V, [(2, a + s, m - s), (3, a, m)], "vg%d" % c)):
+            for t, b, w in jobs:
+                if c in STAGES:
+                    q.wait_ge(S["%s_%d" % (sem, t)], 1)
+                gather(q, t, b, b // 16, w, done)
         V.wait_ge(S["vg%d" % c], 2)
         V.wait_ge(S["sg%d" % c], 3 if s else 2)
         V.quantize_mx(T.qc[:, a:a + n], T.qp[:, a:a + n], T.tile[:, 4 * a:4 * (a + n)]).then_inc(S["q%d" % c], 1)
+    for q, ts, done in ((A, (0, 1), "s_own"), (V, (2, 3), "v_own")):
+        for t in ts:
+            q.wait_ge(S["so%d" % t], 1)
+            gather(q, t, OWN, (N - 1) * LW, CAPP, done)
+    V.wait_ge(S.s_own, 2)
+    V.wait_ge(S.v_own, 2)
+    a, k = own_place(rank)
+    V.quantize_mx(T.onc[:, k:k + 128], T.onp[:, k:k + 128], T.tile[:, 4 * a:4 * (a + 128)]).then_inc(S.q_own, 1)
     V.wait_ge(S.ld_qd, 16)
     V.quantize_mx(T.dc[:], T.dp[:], T.qdsb[:]).then_inc(S.qd_q, 1)
     V.wait_ge(S.ld_od, 16)
     V.tensor_copy(T.odof[:], T.odsb[:]).then_inc(S.odv, 1)
 
     P = g.tensor
-
-    def products(k, rc, rp, c0, n, name):
-        for b in range(NB):
-            o = 512 * (2 * k + b)
-            P.matmul_mx(T.ps[:, o:o + n], T.dc[:, 128 * b:128 * b + 128], T.dp[:, 128 * b:128 * b + 128],
-                        rc[:, c0:c0 + n], rp[:, c0:c0 + n], True, True).then_inc(S["mm_%s%d" % (name, b)], 1)
-
-    w_off = CAPP * NF // 2
-    lead = 128 - CAPP
-    P.wait_ge(S["q%d" % LAST], 1)
+    fa = CAPP * min(off_chip(rank).index(r) for r in far[:2])
+    where = {"n": ("on", 0, CAPP * min(near[:2])),
+             "m": ("on", PAIR + (0 if near[2] < rank else PAD), CAPP * min(near[2], rank)),
+             "a": ("of", fa, CAPP * min(far) + fa), "b": ("of", PAIR - fa, CAPP * min(far) + PAIR - fa)}
     P.wait_ge(S.qd_q, 1)
-    products(0, T.qc, T.qp, N * CAPP - 128, 128, "self")
-    P.wait_ge(S.arr_on, 4 + 4 + 8 + 2 + 2 + 4)
-    products(1, T.onc, T.onp, 0, CAPP * NN, "on")
-    P.wait_ge(S.arr_off, 8 + 4 + 2 + 2 + 2 * NF)
-    products(2, T.ofc, T.ofp, 0, w_off, "offa")
-    products(3, T.ofc, T.ofp, w_off, w_off, "offb")
+    for j, x in enumerate(PRODUCTS):
+        buf, c0, _ = where[x]
+        P.wait_ge(S["arr_" + x], due["arr_" + x])
+        if x == "m":
+            P.wait_ge(S.q_own, 1)
+        for b in range(NB):
+            o = 512 * (NB * j + b)
+            P.matmul_mx(T.ps[:, o:o + PAIR], T.dc[:, 128 * b:128 * b + 128], T.dp[:, 128 * b:128 * b + 128],
+                        T[buf + "c"][:, c0:c0 + PAIR], T[buf + "p"][:, c0:c0 + PAIR],
+                        True, True).then_inc(S["mm_%s%d" % (x, b)], 1)
 
-    def copies(b, wait, put):
-        z = T["z%d" % b]
-        n = 1
-        wait(S["mm_self%d" % b], 1)
-        o = 512 * b + lead
-        put(z[:, CAPP * rank:CAPP * rank + CAPP], T.ps[:, o:o + CAPP])
-        wait(S["mm_on%d" % b], 1)
-        o = 512 * (2 + b)
-        low = [q for q in sorted(near) if q < rank]
-        high = [q for q in sorted(near) if q > rank]
-        for part, first in ((low, 0), (high, len(low))):
-            if part:
-                w = CAPP * len(part)
-                put(z[:, CAPP * part[0]:CAPP * part[0] + w], T.ps[:, o + CAPP * first:o + CAPP * first + w])
-                n += 1
-        f0 = CAPP * min(far)
-        for k, name in ((2, "offa"), (3, "offb")):
-            wait(S["mm_%s%d" % (name, b)], 1)
-            o = 512 * (2 * k + b)
-            put(z[:, f0:f0 + w_off], T.ps[:, o:o + w_off])
-            f0 += w_off
-            n += 1
-        wait(S["cp%d" % b], n)
-        wait(S.odv, 1)
+    def copies(b, q, put):
+        for j, x in enumerate(PRODUCTS):
+            q.wait_ge(S["mm_%s%d" % (x, b)], 1)
+            o, k = 512 * (NB * j + b), where[x][2]
+            put(T["z%d" % b][:, k:k + PAIR], T.ps[:, o:o + PAIR])
+        q.wait_ge(S["cp%d" % b], len(PRODUCTS))
+        q.wait_ge(S.odv, 1)
 
-    copies(0, V.wait_ge, lambda out, src: V.tensor_copy(out, src).then_inc(S.cp0, 1))
-    copies(1, A.wait_ge, lambda out, src: A.activation(out, src, COPY).then_inc(S.cp1, 1))
+    copies(0, V, lambda out, src: V.tensor_copy(out, src).then_inc(S.cp0, 1))
+    copies(1, A, lambda out, src: A.activation(out, src, COPY).then_inc(S.cp1, 1))
     for h, (k0, k1) in enumerate(PIECES):
         picks = T.odof[:, k0 // 16:k1 // 16]
         V.tensor_copy(T.y0[:, k0:k1], T.z0[:].indirect(picks)).then_inc(S["gy0%d" % h], 1)
         A.activation(T.y1[:, k0:k1], T.z1[:].indirect(picks), COPY).then_inc(S["gy1%d" % h], 1)
     for h, (k0, k1) in enumerate(PIECES):
-        for b in range(2):
+        for b in range(NB):
             q = A if (b == 1 and h == 1) else g.sync
             q.wait_ge(S["gy%d%d" % (b, h)], 1)
             q.dma_start(T.y[:, KK * b + k0:KK * b + k1], T["y%d" % b][:, k0:k1]).then_inc(S.st, 16)
     g.sync.wait_ge(S.st, 64)
-
-
-def helper(g, T, r, core, topo, far, peer, bits, send, list_place, off_place):
-    cores, S = T.cores, T.sem
-    es = topo.engines(core, cores[far[0]])
-    g.wait_ge(S.hl, 2)
-    g.remote_dma_fused([send(cores[peer], bits(es), S.list2, T.hlst[:], list_place(r, peer))], local_sem=S.sent)
-    g.wait_ge(S.hp, 8)
-    g.remote_dma_fused([send(cores[d], bits(es[2 * k:2 * k + 2]), S.arr_off, T.hpl[:, CAPP * k:CAPP * k + CAPP],
-                             off_place(T.ofp, r, d)) for k, d in enumerate(far)], local_sem=S.sent)
-    g.wait_ge(S.sent, 8 + 8)

from concourse.bass import DstId, RemoteDMATransfer
from concourse.mybir import AluOpType, ActivationFunctionType, dt

N, CAPP, TK, NB, KK = 8, 96, 1024, 2, 512
LW = CAPP // 16
COPY = ActivationFunctionType.Copy
U8 = dt.uint8
NF, NN = 4, 3
PAIR = 2 * CAPP
PAD = 128 - CAPP
PADC = (N - 1) * CAPP
OWN = PADC + PAD
COLS = OWN + CAPP + PAD

TILE = ["f0", "f2", "f1", "f3", "n0", "n1", "n2"]
CHUNKS = ((0, 192, 64), (192, 192, 64), (384, 192, 64), (576, 128, 0))
STAGES = {0: (0, 4, "la"), 2: (4, 6, "lb"), 3: (6, 7, "lh")}
LISTS = [[("f0", "f0.2"), ("f1", "f2.2"), ("f2", "f4.2"), ("f3", "f6.2")],
         [("n0", "n0.2"), ("n1", "n2.2"), ("n2", "n4.4")]]
CALLS = [(0, [("hc", 0, "n0.8"), ("fc", 2, "f0.8")]), (0, [("hp", 0, "n0.8"), ("fp", 2, "f0.8")]),
         (1, [("hc", 1, "n0.8"), ("fc", 3, "f0.8")]), (1, [("fp", 1, "f0.4"), ("fp", 3, "f4.4")]),
         (2, [("nc", 0, "n0.4"), ("nc", 1, "n4.4")]), (2, [("np", 0, "n0.4"), ("np", 1, "n4.4")]),
         (3, [("nc", 2, "n0.8")]), (3, [("np", 2, "n0.8")])]
HELP = [("hc0", [("fc", 0, "f0.8")]), ("hp0", [("fp", 0, "f0.8")]), ("hc1", [("fc", 1, "f0.8")])]
PRODUCTS = "nmba"
PIECES = ((0, 160), (160, KK))

SCRATCH = {
    "rqsb": ("sbuf", [128, N * LW], "int32"),
    "lst": ("sbuf", [128, (N - 1) * LW], "int32"),
    "kysb": ("sbuf", [128, 4 * TK], "bfloat16"),
    "qdsb": ("sbuf", [128, NB * 512], "bfloat16"),
    "odsb": ("sbuf", [128, KK // 16], "int32"),
    "odof": ("sbuf", [128, KK // 16], "uint16"),
    "tile": ("sbuf", [128, 4 * COLS], "bfloat16"),
    "qc": ("sbuf", [128, PADC + PAD], "float8_e4m3fn_x4"),
    "qp": ("sbuf", [128, PADC + PAD], "uint8"),
    "dc": ("sbuf", [128, NB * 128], "float8_e4m3fn_x4"),
    "dp": ("sbuf", [128, NB * 128], "uint8"),
    "onc": ("sbuf", [128, 2 * PAIR + PAD], "float8_e4m3fn_x4"),
    "onp": ("sbuf", [128, 2 * PAIR + PAD], "uint8"),
    "ofc": ("sbuf", [128, NF * CAPP], "float8_e4m3fn_x4"),
    "ofp": ("sbuf", [128, NF * CAPP], "uint8"),
    "hlst": ("sbuf", [128, LW], "int32"),
    "hcd": ("sbuf", [128, PAIR], "float8_e4m3fn_x4"),
    "hpl": ("sbuf", [128, PAIR], "uint8"),
    "z0": ("sbuf", [128, N * CAPP], "float32"),
    "z1": ("sbuf", [128, N * CAPP], "float32"),
    "y0": ("sbuf", [128, KK], "float32"),
    "y1": ("sbuf", [128, KK], "float32"),
    "ps": ("psum", [128, 512 * 8], "float32"),
}
for _t in range(4):
    SCRATCH["off%d" % _t] = ("sbuf", [128, N * LW], "uint16")

SEMAPHORES = (["ld_rq", "ld_ky", "ld_qd", "ld_od", "la", "lb", "lh", "hl", "hc0", "hc1", "hp0", "sent",
               "arr_n", "arr_m", "arr_a", "arr_b", "qd_q", "odv", "pad", "q_own", "v_own", "s_own"]
              + ["%s%d" % (k, t) for k in ("so", "la_", "lb_", "lh_") for t in range(4)]
              + ["%s%d" % (k, c) for k in ("vg", "sg", "q") for c in range(len(CHUNKS))]
              + ["mm_%s%d" % (k, b) for k in "nmab" for b in range(NB)]
              + ["cp0", "cp1"] + ["gy%d%d" % (b, h) for b in range(NB) for h in range(2)] + ["st"])


def rank_program(g, core, T, topo):
    cores, S = T.cores, T.sem

    def on_chip(r):
        return [q for q in range(N) if topo.chip(cores[q]) == topo.chip(cores[r])]

    def off_chip(r):
        return [q for q in range(N) if topo.chip(cores[q]) != topo.chip(cores[r])]

    def far_of(r):
        i, o = on_chip(r).index(r), off_chip(r)
        return [o[i ^ k] for k in range(NF)]

    def near_of(r):
        i, o = on_chip(r).index(r), on_chip(r)
        return [o[i ^ k] for k in (2, 3, 1)]

    def peer(r, name):
        return (far_of(r) if name[0] == "f" else near_of(r))[int(name[1])]

    def helper_of(r):
        other = [c for c in topo.cores_of(cores[r]) if topo.die(c) != topo.die(cores[r])]
        return other[on_chip(r).index(r)]

    rank = T.rank_of(core)
    mine = [r for r in range(N) if helper_of(r) == core]
    if rank is None and not mine:
        return
    home = mine[0] if rank is None else rank
    far, near = far_of(home), near_of(home)

    pool = {"f": topo.engines(core, cores[far[0]])}
    pool["n"] = [e for e in topo.engines(core, cores[near[0]]) if e not in pool["f"]]

    def count(es):
        return int(es.split(".")[1])

    sent = [0]

    def send(dst, es, sem, src, out):
        first, n = int(es[1:].split(".")[0]), count(es)
        rid, pid, _ = topo.addr(dst)
        sent[0] += n
        return RemoteDMATransfer(dst_ids=[DstId(rid=rid, pnc=pid)],
                                 dma_engine_mask=sum(1 << e for e in pool[es[0]][first:first + n]),
                                 remote_sem=S[sem], srcs=[src], dsts=[out])

    def list_place(r, d):
        k = LW * [peer(d, x) for x in TILE].index(r)
        return T.lst[:, k:k + LW]

    def own_place(d):
        return (OWN, PAIR + CAPP) if near_of(d)[2] < d else (PADC, PAIR)

    def place(kind, r, d):
        if kind[0] == "f":
            k = CAPP * off_chip(d).index(r)
        elif r == near_of(d)[2]:
            k = PAIR if r < d else PAIR + PAD + CAPP
        else:
            k = CAPP * sorted(near_of(d)[:2]).index(r)
        return T["o" + kind][:, k:k + CAPP]

    def u8(kind, ap):
        return ap.bitcast(U8) if kind[1] == "c" else ap

    def arrival(kind, k):
        if kind[0] == "h":
            return "%s%d" % (kind, k)
        return "arr_" + (("m" if k == 2 else "n") if kind[0] == "n" else "a" if k < 2 else "b")

    due = {}
    for _, tr in CALLS + HELP:
        for kind, k, es in tr:
            due[arrival(kind, k)] = due.get(arrival(kind, k), 0) + count(es)
    due["la"] = sum(count(es) for x, es in LISTS[0])
    due["lb"] = sum(count(es) for x, es in LISTS[1][:2])
    due["hl"] = count(LISTS[1][2][1])
    due["lh"] = len(pool["f"])

    if rank is None:
        d = near[NN - 1]
        g.wait_ge(S.hl, due["hl"])
        g.remote_dma_fused([send(cores[d], "f0.%d" % due["lh"], "lh", T.hlst[:], list_place(home, d))], local_sem=S.sent)
        for sem, tr in HELP:
            g.wait_ge(S[sem], due[sem])
            g.remote_dma_fused([send(cores[far[k]], es, arrival(kind, k),
                                     u8(kind, (T.hcd if kind == "fc" else T.hpl)[:, CAPP * k:CAPP * k + CAPP]),
                                     u8(kind, place(kind, home, far[k]))) for kind, k, es in tr], local_sem=S.sent)
        g.wait_ge(S.sent, sent[0])
        return
    helper = helper_of(rank)

    g.sync.dma_start(T.rqsb[:], T.rq[:]).then_inc(S.ld_rq, 16)
    g.sync.dma_start(T.kysb[:], T.ky[:]).then_inc(S.ld_ky, 16)
    g.sync.wait_ge(S.la, due["la"])
    g.sync.dma_start(T.qdsb[:], T.qd[:]).then_inc(S.ld_qd, 16)
    g.sync.dma_start(T.odsb[:], T.od[:]).then_inc(S.ld_od, 16)

    def list_send(x, es, sem):
        d = peer(rank, x)
        src = T.rqsb[:, LW * d:LW * d + LW]
        if x == TILE[-1]:
            return send(helper, es, "hl", src, T.hlst[:])
        return send(cores[d], es, sem, src, list_place(rank, d))

    def data_send(kind, k, es):
        buf = T.qc if kind[1] == "c" else T.qp
        name = "%s%d" % ("n" if kind[0] == "n" else "f", k)
        a = CAPP * TILE.index(name)
        src = u8(kind, buf[:, a:a + CAPP])
        if kind[0] == "h":
            out = (T.hcd if kind == "hc" else T.hpl)[:, CAPP * k:CAPP * k + CAPP]
            return send(helper, es, arrival(kind, k), src, u8(kind, out))
        d = peer(rank, name)
        return send(cores[d], es, arrival(kind, k), src, u8(kind, place(kind, rank, d)))

    g.wait_ge(S.ld_rq, 16)
    for row, sem in zip(LISTS, ("la", "lb")):
        g.remote_dma_fused([list_send(x, es, sem) for x, es in row], local_sem=S.sent)
    for c, tr in CALLS:
        g.wait_ge(S["q%d" % c], 1)
        g.remote_dma_fused([data_send(*x) for x in tr], local_sem=S.sent)
    g.wait_ge(S.sent, sent[0])

    V, A = g.vector, g.scalar
    win = T.kysb[:, 0:4 * TK]

    def offsets(col, src, w, name):
        for t in range(4):
            V.tensor_scalar(T["off%d" % t][:, col:col + w], src, 4, t,
                            AluOpType.mult, AluOpType.add).then_inc(S["%s%d" % (name, t)], 1)

    def gather(q, t, a, col, n, sem):
        out, src = T.tile[:, 4 * a + t:4 * (a + n):4], win.indirect(T["off%d" % t][:, col:col + n // 16])
        if q is V:
            V.tensor_copy(out, src).then_inc(S[sem], 1)
        else:
            A.activation(out, src, COPY).then_inc(S[sem], 1)

    for a in (PADC, OWN + CAPP):
        V.memset(T.tile[:, 4 * a:4 * (a + PAD)], 0.0).then_inc(S.pad, 1)
    V.wait_ge(S.ld_rq, 16)
    offsets((N - 1) * LW, T.rqsb[:, LW * rank:LW * rank + LW], LW, "so")
    V.wait_ge(S.pad, 2)
    for c, (a, n, s) in enumerate(CHUNKS):
        if c in STAGES:
            k0, k1, sem = STAGES[c]
            V.wait_ge(S[sem], due[sem])
            offsets(LW * k0, T.lst[:, LW * k0:LW * k1], LW * (k1 - k0), sem + "_")
        if c == 0:
            V.wait_ge(S.ld_ky, 16)
            A.wait_ge(S.ld_ky, 16)
        m = min(a + n, PADC) - a
        for q, jobs, done in ((A, [(0, a, m), (1, a, m)] + ([(2, a, s)] if s else []), "sg%d" % c),
                              (V, [(2, a + s, m - s), (3, a, m)], "vg%d" % c)):
            for t, b, w in jobs:
                if c in STAGES:
                    q.wait_ge(S["%s_%d" % (sem, t)], 1)
                gather(q, t, b, b // 16, w, done)
        V.wait_ge(S["vg%d" % c], 2)
        V.wait_ge(S["sg%d" % c], 3 if s else 2)
        V.quantize_mx(T.qc[:, a:a + n], T.qp[:, a:a + n], T.tile[:, 4 * a:4 * (a + n)]).then_inc(S["q%d" % c], 1)
    for q, ts, done in ((A, (0, 1), "s_own"), (V, (2, 3), "v_own")):
        for t in ts:
            q.wait_ge(S["so%d" % t], 1)
            gather(q, t, OWN, (N - 1) * LW, CAPP, done)
    V.wait_ge(S.s_own, 2)
    V.wait_ge(S.v_own, 2)
    a, k = own_place(rank)
    V.quantize_mx(T.onc[:, k:k + 128], T.onp[:, k:k + 128], T.tile[:, 4 * a:4 * (a + 128)]).then_inc(S.q_own, 1)
    V.wait_ge(S.ld_qd, 16)
    V.quantize_mx(T.dc[:], T.dp[:], T.qdsb[:]).then_inc(S.qd_q, 1)
    V.wait_ge(S.ld_od, 16)
    V.tensor_copy(T.odof[:], T.odsb[:]).then_inc(S.odv, 1)

    P = g.tensor
    fa = CAPP * min(off_chip(rank).index(r) for r in far[:2])
    where = {"n": ("on", 0, CAPP * min(near[:2])),
             "m": ("on", PAIR + (0 if near[2] < rank else PAD), CAPP * min(near[2], rank)),
             "a": ("of", fa, CAPP * min(far) + fa), "b": ("of", PAIR - fa, CAPP * min(far) + PAIR - fa)}
    P.wait_ge(S.qd_q, 1)
    for j, x in enumerate(PRODUCTS):
        buf, c0, _ = where[x]
        P.wait_ge(S["arr_" + x], due["arr_" + x])
        if x == "m":
            P.wait_ge(S.q_own, 1)
        for b in range(NB):
            o = 512 * (NB * j + b)
            P.matmul_mx(T.ps[:, o:o + PAIR], T.dc[:, 128 * b:128 * b + 128], T.dp[:, 128 * b:128 * b + 128],
                        T[buf + "c"][:, c0:c0 + PAIR], T[buf + "p"][:, c0:c0 + PAIR],
                        True, True).then_inc(S["mm_%s%d" % (x, b)], 1)

    def copies(b, q, put):
        for j, x in enumerate(PRODUCTS):
            q.wait_ge(S["mm_%s%d" % (x, b)], 1)
            o, k = 512 * (NB * j + b), where[x][2]
            put(T["z%d" % b][:, k:k + PAIR], T.ps[:, o:o + PAIR])
        q.wait_ge(S["cp%d" % b], len(PRODUCTS))
        q.wait_ge(S.odv, 1)

    copies(0, V, lambda out, src: V.tensor_copy(out, src).then_inc(S.cp0, 1))
    copies(1, A, lambda out, src: A.activation(out, src, COPY).then_inc(S.cp1, 1))
    for h, (k0, k1) in enumerate(PIECES):
        picks = T.odof[:, k0 // 16:k1 // 16]
        V.tensor_copy(T.y0[:, k0:k1], T.z0[:].indirect(picks)).then_inc(S["gy0%d" % h], 1)
        A.activation(T.y1[:, k0:k1], T.z1[:].indirect(picks), COPY).then_inc(S["gy1%d" % h], 1)
    for h, (k0, k1) in enumerate(PIECES):
        for b in range(NB):
            q = A if (b == 1 and h == 1) else g.sync
            q.wait_ge(S["gy%d%d" % (b, h)], 1)
            q.dma_start(T.y[:, KK * b + k0:KK * b + k1], T["y%d" % b][:, k0:k1]).then_inc(S.st, 16)
    g.sync.wait_ge(S.st, 64)
